import numpy as np
CORES = [120,124,248,252,376,380,504,508]
N = 8
GR, GC = 4, 2
L, KA, KB, F = 4, 2, 1, 128
def setup_inputs(rng):
    return {"a": rng.standard_normal((N, 128, KA * 128), dtype=np.float32), "b": rng.standard_normal((N, 128, KB * F), dtype=np.float32)}
def setup_inputs_big(rng):
    d = setup_inputs(rng)
    for k in ("a", "b"): d[k] = (d[k].astype(np.float32) * 1024.0).astype(d[k].dtype)
    return d
def setup_inputs_small(rng):
    d = setup_inputs(rng)
    for k in ("a", "b"): d[k] = (d[k].astype(np.float32) * (1 / 1024.0)).astype(d[k].dtype)
    return d
def setup_inputs_apart(rng):
    d = setup_inputs(rng)
    f = (10.0 ** rng.permutation(np.linspace(-1.5, 1.5, N))).astype(np.float32).reshape(N, 1, 1)
    for k in ("a", "b"): d[k] = (d[k].astype(np.float32) * f).astype(d[k].dtype)
    return d
def reference(a, b):
    A, B = a.astype(np.float64), b.astype(np.float64)
    y = np.zeros((N, 128, F))
    for i in range(GR):
        for j in range(GC):
            for k in range(L):
                At = A[i * GC + k // KA][:, 128 * (k % KA):128 * (k % KA) + 128]
                Bt = B[(k // KB) * GC + j][:, F * (k % KB):F * (k % KB) + F]
                y[i * GC + j] += At.T @ Bt
    return {"y": y.astype(np.float32 if a.dtype != np.float64 else np.float64)}

@@ -1,0 +1,100 @@
+from concourse.bass import DstId, RemoteDMATransfer
+
+GR, GC, KA, P = 4, 2, 2, 128
+
+SCRATCH = {
+    "bd": ("dram", [P, P], "float32"),
+    "rd": ("dram", [P, P], "float32"),
+    "bs": ("sbuf", [P, GR * P], "float32"),
+    "a_own": ("sbuf", [P, KA * P], "float32"),
+    "a_oth": ("sbuf", [P, KA * P], "float32"),
+    "ys": ("sbuf", [P, P], "float32"),
+    "acc": ("psum", [P, P], "float32"),
+}
+SEMAPHORES = ["ld_bd", "ld_bs", "ld_a", "rel", "nb", "dg", "ap", "cp", "mm", "ev", "st", "loc"]
+
+FIRST_HOP_ENGINES = 4
+
+
+def _bits(mask):
+    return [e for e in range(mask.bit_length()) if (mask >> e) & 1]
+
+
+def _pack(engines):
+    m = 0
+    for e in engines:
+        m |= 1 << e
+    return m
+
+
+def _ring(cores, topo):
+    ring = [cores[0]]
+    while len(ring) < len(cores):
+        ring.append([c for c in cores if c not in ring and topo.may_write(ring[-1], c)][0])
+    return ring
+
+
+def rank_program(g, core, T, topo):
+    rank = T.rank_of(core)
+    if rank is None:
+        return
+    S = T.sem
+    row, col = rank // GC, rank % GC
+    column = [T.cores[q * GC + col] for q in range(GR)]
+    partner = T.cores[row * GC + (1 - col)]
+    ring = _ring(column, topo)
+    at = ring.index(core)
+    nxt, prv, dia = ring[(at + 1) % GR], ring[(at - 1) % GR], ring[(at + 2) % GR]
+    k_nxt, k_prv, k_dia = column.index(nxt), column.index(prv), column.index(dia)
+
+    away = _bits(topo.mask(core, nxt) & topo.mask(core, prv))
+    home = [e for e in _bits(topo.mask(core, partner)) if e not in away]
+    first = away[::len(away) // FIRST_HOP_ENGINES]
+
+    def slot(k):
+        return T.bs[:, k * P:(k + 1) * P]
+
+    def send(dst_core, out, in_, engines, sem):
+        rid, pid = topo.addr(dst_core, core)
+        g.remote_dma_fused([RemoteDMATransfer(dst_ids=[DstId(rid=rid, pnc=pid)], dma_engine_mask=_pack(engines),
+                                              remote_sem=sem, src=in_, dst=out)], local_sem=S.loc)
+        return len(engines)
+
+    g.sync.dma_start(T.bd[:], T.b[:]).then_inc(S.ld_bd, 16)
+    g.scalar.dma_start(T.a_own[:], T.a[:]).then_inc(S.ld_a, 16)
+    g.sync.dma_start(slot(row), T.b[:]).then_inc(S.ld_bs, 16)
+
+    left = 0
+    g.wait_ge(S.ld_bd, 16)
+    left += send(nxt, T.rd[:], T.bd[:], first, S.rel)
+    g.wait_ge(S.ld_a, 16)
+    left += send(partner, T.a_oth[:], T.a_own[:], home, S.ap)
+    left += send(prv, slot(row), T.bd[:], away, S.nb)
+    g.wait_ge(S.rel, len(first))
+    left += send(nxt, slot(k_prv), T.rd[:], away, S.dg)
+    g.wait_ge(S.loc, left)
+
+    g.scalar.wait_ge(S.rel, len(first))
+    g.scalar.dma_start(slot(k_prv), T.rd[:]).then_inc(S.cp, 16)
+
+    need_b = {row: (S.ld_bs, 16), k_nxt: (S.nb, len(away)), k_prv: (S.cp, 16), k_dia: (S.dg, len(away))}
+    need_a = {True: ("ld_a", S.ld_a, 16), False: ("ap", S.ap, len(home))}
+    seen = []
+    order = [row, k_nxt, k_prv, k_dia]
+    for n, k in enumerate(order):
+        mine = (k // KA == col)
+        name, sem, val = need_a[mine]
+        if name not in seen:
+            seen.append(name)
+            g.tensor.wait_ge(sem, val)
+        g.tensor.wait_ge(*need_b[k])
+        abuf = T.a_own if mine else T.a_oth
+        t = k % KA
+        mmi = g.tensor.matmul(T.acc[:], abuf[:, t * P:(t + 1) * P], slot(k), n == 0, n == len(order) - 1)
+    mmi.then_inc(S.mm, 1)
+
+    g.vector.wait_ge(S.mm, 1)
+    g.vector.tensor_copy(T.ys[:], T.acc[:]).then_inc(S.ev, 1)
+    g.sync.wait_ge(S.ev, 1)
+    g.sync.dma_start(T.y[:], T.ys[:]).then_inc(S.st, 16)
+    g.sync.wait_ge(S.st, 16)

@@ -1,19 +1,18 @@
 from concourse.bass import DstId, RemoteDMATransfer
 
 GR, GC, KA, P = 4, 2, 2, 128
+H = P // 2
 
 SCRATCH = {
-    "bd": ("dram", [P, P], "float32"),
-    "rd": ("dram", [P, P], "float32"),
+    "bd": ("dram", [2, P, H], "float32"),
+    "rd": ("dram", [2, P, H], "float32"),
     "bs": ("sbuf", [P, GR * P], "float32"),
     "a_own": ("sbuf", [P, KA * P], "float32"),
     "a_oth": ("sbuf", [P, KA * P], "float32"),
     "ys": ("sbuf", [P, P], "float32"),
     "acc": ("psum", [P, P], "float32"),
 }
-SEMAPHORES = ["ld_bd", "ld_bs", "ld_a", "rel", "nb", "dg", "ap", "cp", "mm", "ev", "st", "loc"]
-
-FIRST_HOP_ENGINES = 4
+SEMAPHORES = ["ld_b0", "ld_b1", "ld_bs", "ld_a", "rel0", "rel1", "nb", "dg", "ap", "cp", "mm", "ev", "st", "loc"]
 
 
 def _bits(mask):
@@ -27,13 +26,6 @@ def _pack(engines):
     return m
 
 
-def _ring(cores, topo):
-    ring = [cores[0]]
-    while len(ring) < len(cores):
-        ring.append([c for c in cores if c not in ring and topo.may_write(ring[-1], c)][0])
-    return ring
-
-
 def rank_program(g, core, T, topo):
     rank = T.rank_of(core)
     if rank is None:
@@ -42,17 +34,21 @@ def rank_program(g, core, T, topo):
     row, col = rank // GC, rank % GC
     column = [T.cores[q * GC + col] for q in range(GR)]
     partner = T.cores[row * GC + (1 - col)]
-    ring = _ring(column, topo)
-    at = ring.index(core)
-    nxt, prv, dia = ring[(at + 1) % GR], ring[(at - 1) % GR], ring[(at + 2) % GR]
-    k_nxt, k_prv, k_dia = column.index(nxt), column.index(prv), column.index(dia)
+    near = [c for c in column if c != core and topo.may_write(core, c)]
+    mate = [c for c in near if topo.rack(topo.host(c)) == topo.rack(topo.host(core))][0]
+    far = [c for c in near if c != mate][0]
+    dia = [c for c in column if c != core and not topo.may_write(core, c)][0]
+    k_far, k_mate, k_dia = column.index(far), column.index(mate), column.index(dia)
 
-    away = _bits(topo.mask(core, nxt) & topo.mask(core, prv))
+    away = _bits(topo.mask(core, far) & topo.mask(core, mate))
     home = [e for e in _bits(topo.mask(core, partner)) if e not in away]
-    first = away[::len(away) // FIRST_HOP_ENGINES]
+    first, rest = away[0::2], away[1::2]
 
     def slot(k):
         return T.bs[:, k * P:(k + 1) * P]
+
+    def half(k, h):
+        return T.bs[:, k * P + h * H:k * P + (h + 1) * H]
 
     def send(dst_core, out, in_, engines, sem):
         rid, pid = topo.addr(dst_core, core)
@@ -60,27 +56,35 @@ def rank_program(g, core, T, topo):
                                               remote_sem=sem, src=in_, dst=out)], local_sem=S.loc)
         return len(engines)
 
-    g.sync.dma_start(T.bd[:], T.b[:]).then_inc(S.ld_bd, 16)
-    g.scalar.dma_start(T.a_own[:], T.a[:]).then_inc(S.ld_a, 16)
+    g.sync.dma_start(T.bd[0], T.b[:, 0:H]).then_inc(S.ld_b0, 16)
+    g.scalar.dma_start(T.bd[1], T.b[:, H:P]).then_inc(S.ld_b1, 16)
     g.sync.dma_start(slot(row), T.b[:]).then_inc(S.ld_bs, 16)
+    g.scalar.dma_start(T.a_own[:], T.a[:]).then_inc(S.ld_a, 16)
 
     left = 0
-    g.wait_ge(S.ld_bd, 16)
-    left += send(nxt, T.rd[:], T.bd[:], first, S.rel)
+    g.wait_ge(S.ld_b0, 16)
+    left += send(far, T.rd[0], T.bd[0], first, S.rel0)
+    g.wait_ge(S.ld_b1, 16)
+    left += send(far, T.rd[1], T.bd[1], first, S.rel1)
+    g.wait_ge(S.ld_bs, 16)
+    left += send(mate, slot(row), slot(row), rest, S.nb)
     g.wait_ge(S.ld_a, 16)
     left += send(partner, T.a_oth[:], T.a_own[:], home, S.ap)
-    left += send(prv, slot(row), T.bd[:], away, S.nb)
-    g.wait_ge(S.rel, len(first))
-    left += send(nxt, slot(k_prv), T.rd[:], away, S.dg)
+    g.wait_ge(S.rel0, len(first))
+    left += send(mate, half(k_far, 0), T.rd[0], away, S.dg)
+    g.wait_ge(S.rel1, len(first))
+    left += send(mate, half(k_far, 1), T.rd[1], away, S.dg)
     g.wait_ge(S.loc, left)
 
-    g.scalar.wait_ge(S.rel, len(first))
-    g.scalar.dma_start(slot(k_prv), T.rd[:]).then_inc(S.cp, 16)
+    g.scalar.wait_ge(S.rel0, len(first))
+    g.scalar.dma_start(half(k_far, 0), T.rd[0]).then_inc(S.cp, 16)
+    g.scalar.wait_ge(S.rel1, len(first))
+    g.scalar.dma_start(half(k_far, 1), T.rd[1]).then_inc(S.cp, 16)
 
-    need_b = {row: (S.ld_bs, 16), k_nxt: (S.nb, len(away)), k_prv: (S.cp, 16), k_dia: (S.dg, len(away))}
+    need_b = {row: (S.ld_bs, 16), k_mate: (S.nb, len(rest)), k_far: (S.cp, 32), k_dia: (S.dg, 2 * len(away))}
     need_a = {True: ("ld_a", S.ld_a, 16), False: ("ap", S.ap, len(home))}
     seen = []
-    order = [row, k_nxt, k_prv, k_dia]
+    order = [row, k_mate, k_far, k_dia]
     for n, k in enumerate(order):
         mine = (k // KA == col)
         name, sem, val = need_a[mine]

@@ -1,18 +1,24 @@
 from concourse.bass import DstId, RemoteDMATransfer
 
 GR, GC, KA, P = 4, 2, 2, 128
-H = P // 2
+C0 = 76
+CB = [0, C0, P]
+BANK = 512
 
 SCRATCH = {
-    "bd": ("dram", [2, P, H], "float32"),
-    "rd": ("dram", [2, P, H], "float32"),
+    "bd0": ("dram", [P, C0], "float32"),
+    "bd1": ("dram", [P, P - C0], "float32"),
+    "rd0": ("dram", [P, C0], "float32"),
+    "rd1": ("dram", [P, P - C0], "float32"),
     "bs": ("sbuf", [P, GR * P], "float32"),
     "a_own": ("sbuf", [P, KA * P], "float32"),
     "a_oth": ("sbuf", [P, KA * P], "float32"),
     "ys": ("sbuf", [P, P], "float32"),
-    "acc": ("psum", [P, P], "float32"),
+    "acc0": ("psum", [P, BANK], "float32"),
+    "acc1": ("psum", [P, BANK], "float32"),
 }
-SEMAPHORES = ["ld_b0", "ld_b1", "ld_bs", "ld_a", "rel0", "rel1", "nb", "dg", "ap", "cp", "mm", "ev", "st", "loc"]
+SEMAPHORES = ["ld_b0", "ld_b1", "ld_bs", "ld_a", "rel0", "rel1", "nb", "dg0", "dg1", "ap", "cp0", "cp1",
+              "mm0", "mm1", "ev0", "ev1", "st0", "st1", "loc"]
 
 
 def _bits(mask):
@@ -42,13 +48,16 @@ def rank_program(g, core, T, topo):
 
     away = _bits(topo.mask(core, far) & topo.mask(core, mate))
     home = [e for e in _bits(topo.mask(core, partner)) if e not in away]
-    first, rest = away[0::2], away[1::2]
+    cable = away[0::4]
+    spare = away[2::4]
+    rest = away[1::2]
+    inchip = spare + home[:len(home) - len(spare)]
 
     def slot(k):
         return T.bs[:, k * P:(k + 1) * P]
 
-    def half(k, h):
-        return T.bs[:, k * P + h * H:k * P + (h + 1) * H]
+    def piece(k, h):
+        return T.bs[:, k * P + CB[h]:k * P + CB[h + 1]]
 
     def send(dst_core, out, in_, engines, sem):
         rid, pid = topo.addr(dst_core, core)
@@ -56,49 +65,59 @@ def rank_program(g, core, T, topo):
                                               remote_sem=sem, src=in_, dst=out)], local_sem=S.loc)
         return len(engines)
 
-    g.sync.dma_start(T.bd[0], T.b[:, 0:H]).then_inc(S.ld_b0, 16)
-    g.scalar.dma_start(T.bd[1], T.b[:, H:P]).then_inc(S.ld_b1, 16)
+    g.sync.dma_start(T.bd0[:], T.b[:, 0:C0]).then_inc(S.ld_b0, 16)
+    g.scalar.dma_start(T.bd1[:], T.b[:, C0:P]).then_inc(S.ld_b1, 16)
     g.sync.dma_start(slot(row), T.b[:]).then_inc(S.ld_bs, 16)
     g.scalar.dma_start(T.a_own[:], T.a[:]).then_inc(S.ld_a, 16)
 
     left = 0
     g.wait_ge(S.ld_b0, 16)
-    left += send(far, T.rd[0], T.bd[0], first, S.rel0)
+    left += send(far, T.rd0[:], T.bd0[:], cable, S.rel0)
     g.wait_ge(S.ld_b1, 16)
-    left += send(far, T.rd[1], T.bd[1], first, S.rel1)
+    left += send(far, T.rd1[:], T.bd1[:], cable, S.rel1)
     g.wait_ge(S.ld_bs, 16)
     left += send(mate, slot(row), slot(row), rest, S.nb)
     g.wait_ge(S.ld_a, 16)
-    left += send(partner, T.a_oth[:], T.a_own[:], home, S.ap)
-    g.wait_ge(S.rel0, len(first))
-    left += send(mate, half(k_far, 0), T.rd[0], away, S.dg)
-    g.wait_ge(S.rel1, len(first))
-    left += send(mate, half(k_far, 1), T.rd[1], away, S.dg)
+    left += send(partner, T.a_oth[:], T.a_own[:], inchip, S.ap)
+    g.wait_ge(S.rel0, len(cable))
+    left += send(mate, piece(k_far, 0), T.rd0[:], away, S.dg0)
+    g.wait_ge(S.rel1, len(cable))
+    left += send(mate, piece(k_far, 1), T.rd1[:], away, S.dg1)
     g.wait_ge(S.loc, left)
 
-    g.scalar.wait_ge(S.rel0, len(first))
-    g.scalar.dma_start(half(k_far, 0), T.rd[0]).then_inc(S.cp, 16)
-    g.scalar.wait_ge(S.rel1, len(first))
-    g.scalar.dma_start(half(k_far, 1), T.rd[1]).then_inc(S.cp, 16)
+    g.scalar.wait_ge(S.rel0, len(cable))
+    g.scalar.dma_start(piece(k_far, 0), T.rd0[:]).then_inc(S.cp0, 16)
+    g.scalar.wait_ge(S.rel1, len(cable))
+    g.scalar.dma_start(piece(k_far, 1), T.rd1[:]).then_inc(S.cp1, 16)
 
-    need_b = {row: (S.ld_bs, 16), k_mate: (S.nb, len(rest)), k_far: (S.cp, 32), k_dia: (S.dg, 2 * len(away))}
-    need_a = {True: ("ld_a", S.ld_a, 16), False: ("ap", S.ap, len(home))}
+    acc = [T.acc0[:, 0:C0], T.acc1[:, 0:P - C0]]
+    need_b = {(row, 0): ("ld_bs", S.ld_bs, 16), (row, 1): ("ld_bs", S.ld_bs, 16),
+              (k_mate, 0): ("nb", S.nb, len(rest)), (k_mate, 1): ("nb", S.nb, len(rest)),
+              (k_far, 0): ("cp0", S.cp0, 16), (k_far, 1): ("cp1", S.cp1, 16),
+              (k_dia, 0): ("dg0", S.dg0, len(away)), (k_dia, 1): ("dg1", S.dg1, len(away))}
+    need_a = {True: ("ld_a", S.ld_a, 16), False: ("ap", S.ap, len(inchip))}
+    done = [S.mm0, S.mm1]
     seen = []
-    order = [row, k_mate, k_far, k_dia]
-    for n, k in enumerate(order):
+    order = [(row, 0), (row, 1), (k_mate, 0), (k_mate, 1), (k_far, 0), (k_dia, 0), (k_far, 1), (k_dia, 1)]
+    for k, h in order:
         mine = (k // KA == col)
-        name, sem, val = need_a[mine]
-        if name not in seen:
-            seen.append(name)
-            g.tensor.wait_ge(sem, val)
-        g.tensor.wait_ge(*need_b[k])
+        for name, sem, val in (need_a[mine], need_b[(k, h)]):
+            if name not in seen:
+                seen.append(name)
+                g.tensor.wait_ge(sem, val)
         abuf = T.a_own if mine else T.a_oth
         t = k % KA
-        mmi = g.tensor.matmul(T.acc[:], abuf[:, t * P:(t + 1) * P], slot(k), n == 0, n == len(order) - 1)
-    mmi.then_inc(S.mm, 1)
+        mmi = g.tensor.matmul(acc[h], abuf[:, t * P:(t + 1) * P], piece(k, h), k == row, k == k_dia)
+        if k == k_dia:
+            mmi.then_inc(done[h], 1)
 
-    g.vector.wait_ge(S.mm, 1)
-    g.vector.tensor_copy(T.ys[:], T.acc[:]).then_inc(S.ev, 1)
-    g.sync.wait_ge(S.ev, 1)
-    g.sync.dma_start(T.y[:], T.ys[:]).then_inc(S.st, 16)
-    g.sync.wait_ge(S.st, 16)
+    g.vector.wait_ge(S.mm0, 1)
+    g.vector.tensor_copy(T.ys[:, 0:C0], acc[0]).then_inc(S.ev0, 1)
+    g.vector.wait_ge(S.mm1, 1)
+    g.vector.tensor_copy(T.ys[:, C0:P], acc[1]).then_inc(S.ev1, 1)
+    g.scalar.wait_ge(S.ev0, 1)
+    g.scalar.dma_start(T.y[:, 0:C0], T.ys[:, 0:C0]).then_inc(S.st0, 16)
+    g.sync.wait_ge(S.ev1, 1)
+    g.sync.dma_start(T.y[:, C0:P], T.ys[:, C0:P]).then_inc(S.st1, 16)
+    g.scalar.wait_ge(S.st0, 16)
+    g.sync.wait_ge(S.st1, 16)

from concourse.bass import DstId, RemoteDMATransfer

GR, GC, KA, P = 4, 2, 2, 128
C0 = 76
CB = [0, C0, P]
BANK = 512

SCRATCH = {
    "bd0": ("dram", [P, C0], "float32"),
    "bd1": ("dram", [P, P - C0], "float32"),
    "rd0": ("dram", [P, C0], "float32"),
    "rd1": ("dram", [P, P - C0], "float32"),
    "bs": ("sbuf", [P, GR * P], "float32"),
    "a_own": ("sbuf", [P, KA * P], "float32"),
    "a_oth": ("sbuf", [P, KA * P], "float32"),
    "ys": ("sbuf", [P, P], "float32"),
    "acc0": ("psum", [P, BANK], "float32"),
    "acc1": ("psum", [P, BANK], "float32"),
}
SEMAPHORES = ["ld_b0", "ld_b1", "ld_bs", "ld_a", "rel0", "rel1", "nb", "dg0", "dg1", "ap", "cp0", "cp1",
              "mm0", "mm1", "ev0", "ev1", "st0", "st1", "loc"]


def _bits(mask):
    return [e for e in range(mask.bit_length()) if (mask >> e) & 1]


def _pack(engines):
    m = 0
    for e in engines:
        m |= 1 << e
    return m


def rank_program(g, core, T, topo):
    rank = T.rank_of(core)
    if rank is None:
        return
    S = T.sem
    row, col = rank // GC, rank % GC
    column = [T.cores[q * GC + col] for q in range(GR)]
    partner = T.cores[row * GC + (1 - col)]
    near = [c for c in column if c != core and topo.may_write(core, c)]
    mate = [c for c in near if topo.rack(topo.host(c)) == topo.rack(topo.host(core))][0]
    far = [c for c in near if c != mate][0]
    dia = [c for c in column if c != core and not topo.may_write(core, c)][0]
    k_far, k_mate, k_dia = column.index(far), column.index(mate), column.index(dia)

    away = _bits(topo.mask(core, far) & topo.mask(core, mate))
    home = [e for e in _bits(topo.mask(core, partner)) if e not in away]
    cable = away[0::4]
    spare = away[2::4]
    rest = away[1::2]
    inchip = spare + home[:len(home) - len(spare)]

    def slot(k):
        return T.bs[:, k * P:(k + 1) * P]

    def piece(k, h):
        return T.bs[:, k * P + CB[h]:k * P + CB[h + 1]]

    def send(dst_core, out, in_, engines, sem):
        rid, pid = topo.addr(dst_core, core)
        g.remote_dma_fused([RemoteDMATransfer(dst_ids=[DstId(rid=rid, pnc=pid)], dma_engine_mask=_pack(engines),
                                              remote_sem=sem, src=in_, dst=out)], local_sem=S.loc)
        return len(engines)

    g.sync.dma_start(T.bd0[:], T.b[:, 0:C0]).then_inc(S.ld_b0, 16)
    g.scalar.dma_start(T.bd1[:], T.b[:, C0:P]).then_inc(S.ld_b1, 16)
    g.sync.dma_start(slot(row), T.b[:]).then_inc(S.ld_bs, 16)
    g.scalar.dma_start(T.a_own[:], T.a[:]).then_inc(S.ld_a, 16)

    left = 0
    g.wait_ge(S.ld_b0, 16)
    left += send(far, T.rd0[:], T.bd0[:], cable, S.rel0)
    g.wait_ge(S.ld_b1, 16)
    left += send(far, T.rd1[:], T.bd1[:], cable, S.rel1)
    g.wait_ge(S.ld_bs, 16)
    left += send(mate, slot(row), slot(row), rest, S.nb)
    g.wait_ge(S.ld_a, 16)
    left += send(partner, T.a_oth[:], T.a_own[:], inchip, S.ap)
    g.wait_ge(S.rel0, len(cable))
    left += send(mate, piece(k_far, 0), T.rd0[:], away, S.dg0)
    g.wait_ge(S.rel1, len(cable))
    left += send(mate, piece(k_far, 1), T.rd1[:], away, S.dg1)
    g.wait_ge(S.loc, left)

    g.scalar.wait_ge(S.rel0, len(cable))
    g.scalar.dma_start(piece(k_far, 0), T.rd0[:]).then_inc(S.cp0, 16)
    g.scalar.wait_ge(S.rel1, len(cable))
    g.scalar.dma_start(piece(k_far, 1), T.rd1[:]).then_inc(S.cp1, 16)

    acc = [T.acc0[:, 0:C0], T.acc1[:, 0:P - C0]]
    need_b = {(row, 0): ("ld_bs", S.ld_bs, 16), (row, 1): ("ld_bs", S.ld_bs, 16),
              (k_mate, 0): ("nb", S.nb, len(rest)), (k_mate, 1): ("nb", S.nb, len(rest)),
              (k_far, 0): ("cp0", S.cp0, 16), (k_far, 1): ("cp1", S.cp1, 16),
              (k_dia, 0): ("dg0", S.dg0, len(away)), (k_dia, 1): ("dg1", S.dg1, len(away))}
    need_a = {True: ("ld_a", S.ld_a, 16), False: ("ap", S.ap, len(inchip))}
    done = [S.mm0, S.mm1]
    seen = []
    order = [(row, 0), (row, 1), (k_mate, 0), (k_mate, 1), (k_far, 0), (k_dia, 0), (k_far, 1), (k_dia, 1)]
    for k, h in order:
        mine = (k // KA == col)
        for name, sem, val in (need_a[mine], need_b[(k, h)]):
            if name not in seen:
                seen.append(name)
                g.tensor.wait_ge(sem, val)
        abuf = T.a_own if mine else T.a_oth
        t = k % KA
        mmi = g.tensor.matmul(acc[h], abuf[:, t * P:(t + 1) * P], piece(k, h), k == row, k == k_dia)
        if k == k_dia:
            mmi.then_inc(done[h], 1)

    g.vector.wait_ge(S.mm0, 1)
    g.vector.tensor_copy(T.ys[:, 0:C0], acc[0]).then_inc(S.ev0, 1)
    g.vector.wait_ge(S.mm1, 1)
    g.vector.tensor_copy(T.ys[:, C0:P], acc[1]).then_inc(S.ev1, 1)
    g.scalar.wait_ge(S.ev0, 1)
    g.scalar.dma_start(T.y[:, 0:C0], T.ys[:, 0:C0]).then_inc(S.st0, 16)
    g.sync.wait_ge(S.ev1, 1)
    g.sync.dma_start(T.y[:, C0:P], T.ys[:, C0:P]).then_inc(S.st1, 16)
    g.scalar.wait_ge(S.st0, 16)
    g.sync.wait_ge(S.st1, 16)
